import numpy as np
import ml_dtypes


def mxq(x, axis, fmt="e4m3"):
    dtype, down = {"e4m3": (ml_dtypes.float8_e4m3fn, 7), "e5m2": (ml_dtypes.float8_e5m2, 14)}[fmt]
    v = np.moveaxis(np.asarray(x, np.float32).astype(ml_dtypes.bfloat16).astype(np.float64), axis, -1)
    blocks = v.reshape(v.shape[:-1] + (-1, 32))
    amax = np.abs(blocks).max(-1, keepdims=True)
    byte = np.maximum(np.where(amax > 0, np.frexp(amax)[1] - 1 + 127, 0) - down, 1)
    scale = np.exp2(byte - 127.0)
    codes = (blocks / scale).astype(np.float32).astype(dtype).astype(np.float64)
    return np.moveaxis((codes * scale).reshape(v.shape), -1, axis)


WIDE = False


def mx_kscale(k):
    if not WIDE:
        return np.ones(k)
    levels = np.array([10, -10, 5, -5, 0])
    if k % 512:
        return np.exp2(np.random.permutation(np.resize(levels, k // 32))).repeat(32)
    a = np.empty((k // 512, 16))
    for p in range(k // 512):
        a[p, :8] = np.random.permutation(np.resize(levels, 8))
        for g in range(8):
            far = levels[np.abs(levels - a[p, g]) >= 10]
            a[p, g + 8] = far[np.random.randint(len(far))]
    return np.exp2(a.ravel()).repeat(32)


def f64(x):
    return np.asarray(x).astype(np.float64)


def striped(idx):
    return np.tile(idx.reshape(-1, 16).T, (8, 1)).astype(np.uint16)


def unstriped(offs):
    return offs[:16].T.reshape(-1).astype(np.int64)


def pack_weight(w):
    k, n = w.shape
    w = f64(np.asarray(w, np.float32).astype(ml_dtypes.bfloat16)).reshape(k // 32, 32, n)
    amax = np.abs(w).max(1)
    byte = np.clip(np.where(amax > 0, np.frexp(amax)[1] - 1 + 127 - 7, 1), 1, 254)
    scaled = (w * np.exp2(127.0 - byte)[:, None, :]).reshape(k, n).astype(np.float32)
    words = np.ascontiguousarray(scaled.reshape(k // 512, 128, 4, n).transpose(0, 1, 3, 2)).astype(ml_dtypes.float8_e4m3fn).view(np.uint8)
    return words, np.ascontiguousarray(byte.astype(np.uint8).reshape(k // 512, 16, n))


def unpack_weight(words, scales):
    g, p, n, _ = words.shape
    vals = np.ascontiguousarray(words).view(ml_dtypes.float8_e4m3fn).astype(np.float64) * np.repeat(np.exp2(scales.astype(np.float64) - 127.0), 8, axis=1)[..., None]
    return vals.transpose(0, 1, 3, 2).reshape(g * 512, n)


def relu(v):
    return np.maximum(v, 0.0)


K, T, E, C, N = 512, 1024, 24, 128, 256
TOP = 3


def by_expert(wq, xq):
    return np.concatenate([wq[e].T @ xq[:, e * C:(e + 1) * C] for e in range(E)], axis=1)


def setup_inputs():
    n = np.random.standard_normal
    s = mx_kscale(K)[:, None]
    deal = np.repeat(np.arange(E), C).reshape(TOP, T)[:, np.random.permutation(T)]
    deal = np.take_along_axis(deal, np.argsort(np.random.rand(TOP, T), axis=0), axis=0)
    for _ in range(8):
        s_, t_ = np.random.permutation(T).reshape(2, -1); r = np.random.randint(TOP, size=T // 2); x, y = deal[r, s_].copy(), deal[r, t_].copy()
        ok = ~((deal[:, s_] == y).any(0) | (deal[:, t_] == x).any(0)); deal[r[ok], s_[ok]] = y[ok]; deal[r[ok], t_[ok]] = x[ok]
    order = np.lexsort((np.random.rand(TOP * T), deal.reshape(-1)))
    slot_token = order % T; pos = np.empty(TOP * T, np.int64); pos[order] = np.arange(TOP * T); pos = pos.reshape(TOP, T)
    g = np.random.uniform(0.5, 1.5, (TOP, T)); g = g / g.sum(0)
    packed = [pack_weight(m) for m in n((E, K, N)) / np.sqrt(K) / s[None]]
    return {
        "xT": (n((K, T)) * s).astype(np.float32),
        "w_words": np.stack([m[0] for m in packed]),
        "w_scales": np.stack([m[1] for m in packed]),
        "b": (0.3 * n((N, E))).astype(np.float32),
        "gate": np.stack([np.tile(r, (N, 1)) for r in g]).astype(np.float32),
        "offs": striped(slot_token),
        "pos1": striped(pos[0]),
        "pos2": striped(pos[1]),
        "pos3": striped(pos[2]),
    }


def reference(xT, w_words, w_scales, b, gate, offs, pos1, pos2, pos3):
    idx = unstriped(offs)
    w = np.stack([unpack_weight(w_words[e], w_scales[e]) for e in range(E)])
    xq = mxq(f64(xT)[:, idx], 0, "e4m3")
    y = by_expert(w, xq)
    y = relu(y + np.repeat(f64(b), C, axis=1))
    return sum(f64(gate[r]) * y[:, unstriped(p)] for r, p in enumerate((pos1, pos2, pos3)))

@@ -1,0 +1,162 @@
+from contextlib import ExitStack
+
+import concourse.mybir as mybir
+from concourse.masks import make_identity
+
+K, T, E, C, N, R = 512, 1024, 24, 128, 256, 3
+FLOPS = 2 * K * N * E * C
+P = 128
+H = N // P
+
+F32 = mybir.dt.float32
+BF16 = mybir.dt.bfloat16
+U32 = mybir.dt.uint32
+I32 = mybir.dt.int32
+U16 = mybir.dt.uint16
+U8 = mybir.dt.uint8
+FP8X4 = mybir.dt.float8_e4m3fn_x4
+MULT = mybir.AluOpType.mult
+ADD = mybir.AluOpType.add
+COPY = mybir.ActivationFunctionType.Copy
+RELU = mybir.ActivationFunctionType.Relu
+
+X_CHUNKS = (512, 256, 256)
+SCALAR_SHARE = (256, 128, 128)
+W_GROUP = 4
+GATHERS = (6, 6, 6, 4, 2)
+
+
+def tile_moe_tk_lin_relu_kernel(tc, xT, w_words, w_scales, b, gate, offs, pos1, pos2, pos3, out):
+    nc = tc.nc
+    with ExitStack() as ctx:
+        lists = ctx.enter_context(tc.tile_pool(name="lists", bufs=1))
+        keep = ctx.enter_context(tc.tile_pool(name="keep", bufs=1))
+        psum = ctx.enter_context(tc.psum_pool(name="psum", bufs=8))
+
+        offs_t = lists.tile([P, R * T // 16], U16, name="offs_t")
+        pos_t = [lists.tile([P, T // 16], U16, name=f"pos{r}_t") for r in range(R)]
+
+        w_sc = keep.tile([P, E, N], U8, name="w_sc", align_bytes=64)
+        x_codes = keep.tile([P, T], U32, name="x_codes", align_bytes=64)
+        x_scales = keep.tile([P, T], U8, name="x_scales", align_bytes=64)
+        bias = keep.tile([P, H, E], F32, name="bias")
+        warm = keep.tile([P, 1], F32, name="warm")
+        ident = keep.tile([P, P], F32, name="ident")
+
+        nc.vector.memset(warm[:], 0.0)
+        nc.scalar.activation(warm[:], warm[:], RELU)
+        nc.vector.memset(w_sc[:].rearrange("p e n -> p (e n)").bitcast(I32), 0)
+        nc.gpsimd.memset(x_scales[:], 0)
+        make_identity(nc, ident[:])
+
+        x_view = xT.rearrange("(p j) t -> p j t", j=4)
+        x_raw = []
+        t0 = 0
+        for i, width in enumerate(X_CHUNKS):
+            raw = keep.tile([P, 4, width], F32, name=f"x_raw{i}")
+            nc.sync.dma_start(out=raw[:], in_=x_view[:, :, t0 : t0 + width])
+            x_raw.append(raw)
+            t0 += width
+        nc.sync.dma_start(offs_t[:], offs)
+        sc_view = w_scales.rearrange("e a q n -> q (e a) n")
+        for q in range(4):
+            nc.sync.dma_start(
+                out=w_sc[32 * q : 32 * q + 4, :, :].rearrange("p e n -> p (e n)").bitcast(I32).rearrange("p (e n) -> p e n", e=E),
+                in_=sc_view[4 * q : 4 * q + 4].bitcast(I32),
+            )
+        w_view = w_words.rearrange("e a p n r -> p (e a) (n r)")
+        w_t = []
+        for g in range(E // W_GROUP):
+            wt = keep.tile([P, W_GROUP, N], I32, name=f"w{g}", align_bytes=64)
+            nc.sync.dma_start(out=wt[:], in_=w_view[:, g * W_GROUP : (g + 1) * W_GROUP, :].bitcast(I32))
+            w_t.append(wt)
+            if g == 0:
+                nc.sync.dma_start(out=bias[:], in_=b.rearrange("(h p) e -> p h e", p=P))
+        for r, pos in enumerate((pos1, pos2, pos3)):
+            nc.sync.dma_start(pos_t[r][:], pos)
+        gate_t = []
+        for h in range(H):
+            gt = keep.tile([P, R, T], F32, name=f"gate{h}")
+            nc.sync.dma_start(out=gt[:], in_=gate[:, h * P : (h + 1) * P, :].rearrange("r p t -> p r t"))
+            gate_t.append(gt)
+
+        t0 = 0
+        for i, width in enumerate(X_CHUNKS):
+            grouped = keep.tile([P, width, 4], BF16, name=f"grouped{i}", align_bytes=64)
+            cut = width - SCALAR_SHARE[i]
+            nc.vector.tensor_copy(out=grouped[:, :cut, :], in_=x_raw[i][:, :, :cut].rearrange("p j w -> p w j"))
+            nc.scalar.activation(grouped[:, cut:, :], x_raw[i][:, :, cut:].rearrange("p j w -> p w j"), COPY)
+            nc.vector.quantize_mx(
+                out=x_codes[:, t0 : t0 + width].bitcast(FP8X4),
+                scales=x_scales[:, t0 : t0 + width],
+                in_=grouped[:].rearrange("p w j -> p (w j)"),
+            )
+            t0 += width
+
+        y = [keep.tile([P, E * C], F32, name=f"y{h}") for h in range(H)]
+        e0 = 0
+        for i, experts in enumerate(GATHERS):
+            cols = experts * C
+            codes = keep.tile([P, cols], U32, name=f"codes{i}", align_bytes=64)
+            scales = keep.tile([P, cols], U8, name=f"scales{i}", align_bytes=64)
+            slots = offs_t[:, e0 * C // 16 : (e0 + experts) * C // 16]
+            nc.vector.tensor_copy(codes[:], x_codes[:].indirect(slots))
+            nc.vector.tensor_copy(scales[:], x_scales[:].indirect(slots))
+            for h in range(H):
+                for s0 in range(0, experts, 3 if experts % 3 == 0 else 4):
+                    run = range(s0, min(experts, s0 + (3 if experts % 3 == 0 else 4)))
+                    acc = psum.tile([P, 512], F32, name="bank")
+                    for s in run:
+                        e = e0 + s
+                        nc.tensor.matmul_mx(
+                            out=acc[:, (s - s0) * C : (s - s0 + 1) * C],
+                            lhsT=w_t[e // W_GROUP][:, e % W_GROUP, h * P : (h + 1) * P].bitcast(FP8X4),
+                            lhsT_scale=w_sc[:, e, h * P : (h + 1) * P],
+                            rhs=codes[:, s * C : (s + 1) * C].bitcast(FP8X4),
+                            rhs_scale=scales[:, s * C : (s + 1) * C],
+                            start=True,
+                            stop=True,
+                        )
+                    for s in run:
+                        e = e0 + s
+                        nc.scalar.activation(y[h][:, e * C : (e + 1) * C], acc[:, (s - s0) * C : (s - s0 + 1) * C], RELU, bias=bias[:, h, e : e + 1])
+            e0 += experts
+
+        for h in range(H):
+            prod = [keep.tile([P, T], F32, name=f"prod{h}{r}") for r in range(R)]
+            result = keep.tile([P, T], F32, name=f"result{h}")
+
+            def product(r, lo, hi):
+                nc.vector.tensor_tensor(prod[r][:, lo:hi], y[h][:].indirect(pos_t[r][:, lo // 16 : hi // 16]), gate_t[h][:, r, lo:hi], MULT)
+
+            def store(lo, hi):
+                nc.sync.dma_start(out=out[h * P : (h + 1) * P, lo:hi], in_=result[:, lo:hi])
+
+            def tensor_sum(lo, hi):
+                turned = psum.tile([P, 512], F32, name="bank")
+                for j in range(lo // P, hi // P):
+                    for r in range(R):
+                        nc.tensor.matmul(turned[:, j * P - lo : (j + 1) * P - lo], lhsT=prod[r][:, j * P : (j + 1) * P], rhs=ident[:], is_transpose=True, start=(r == 0), stop=(r == R - 1))
+                sums = keep.tile([P, hi - lo], F32, name=f"sums{h}{lo}")
+                nc.scalar.activation(sums[:], turned[:, : hi - lo], COPY)
+                back = psum.tile([P, 512], F32, name="bank")
+                for j in range((hi - lo) // P):
+                    nc.tensor.transpose(back[:, j * P : (j + 1) * P], sums[:, j * P : (j + 1) * P], ident[:])
+                nc.scalar.activation(result[:, lo:hi], back[:, : hi - lo], COPY)
+                store(lo, hi)
+
+            edge = T if h == 0 else 768
+            for r in range(2):
+                product(r, 0, edge)
+            cuts = [0, 512, edge]
+            for lo, hi in zip(cuts[:-1], cuts[1:]):
+                product(2, lo, hi)
+                tensor_sum(lo, hi)
+            if h == 1:
+                half_sum = keep.tile([P, T - edge], F32, name="half_sum")
+                product(0, edge, T)
+                product(1, edge, T)
+                product(2, edge, T)
+                nc.vector.tensor_tensor(half_sum[:], prod[0][:, edge:], prod[1][:, edge:], ADD)
+                nc.vector.tensor_tensor(result[:, edge:], half_sum[:], prod[2][:, edge:], ADD)
+                store(edge, T)

@@ -20,10 +20,10 @@ ADD = mybir.AluOpType.add
 COPY = mybir.ActivationFunctionType.Copy
 RELU = mybir.ActivationFunctionType.Relu
 
-X_CHUNKS = (512, 256, 256)
-SCALAR_SHARE = (256, 128, 128)
+X_CHUNKS = (256, 512, 256)
+SCALAR_SHARE = (64, 144, 64)
 W_GROUP = 4
-GATHERS = (6, 6, 6, 4, 2)
+GATHERS = (6, 6, 6, 5, 1)
 
 
 def tile_moe_tk_lin_relu_kernel(tc, xT, w_words, w_scales, b, gate, offs, pos1, pos2, pos3, out):
@@ -72,20 +72,18 @@ def tile_moe_tk_lin_relu_kernel(tc, xT, w_words, w_scales, b, gate, offs, pos1, 
             w_t.append(wt)
             if g == 0:
                 nc.sync.dma_start(out=bias[:], in_=b.rearrange("(h p) e -> p h e", p=P))
+        gate_t = [keep.tile([P, R, T], F32, name=f"gate{h}") for h in range(H)]
         for r, pos in enumerate((pos1, pos2, pos3)):
             nc.sync.dma_start(pos_t[r][:], pos)
-        gate_t = []
-        for h in range(H):
-            gt = keep.tile([P, R, T], F32, name=f"gate{h}")
-            nc.sync.dma_start(out=gt[:], in_=gate[:, h * P : (h + 1) * P, :].rearrange("r p t -> p r t"))
-            gate_t.append(gt)
+            nc.sync.dma_start(out=gate_t[0][:, r, :], in_=gate[r, 0:P, :])
+        nc.sync.dma_start(out=gate_t[1][:], in_=gate[:, P:N, :].rearrange("r p t -> p r t"))
 
         t0 = 0
         for i, width in enumerate(X_CHUNKS):
             grouped = keep.tile([P, width, 4], BF16, name=f"grouped{i}", align_bytes=64)
             cut = width - SCALAR_SHARE[i]
-            nc.vector.tensor_copy(out=grouped[:, :cut, :], in_=x_raw[i][:, :, :cut].rearrange("p j w -> p w j"))
-            nc.scalar.activation(grouped[:, cut:, :], x_raw[i][:, :, cut:].rearrange("p j w -> p w j"), COPY)
+            nc.vector.tensor_copy(out=grouped[:, :cut, :].rearrange("p (c i) j -> p c j i", i=4), in_=x_raw[i][:, :, :cut].rearrange("p j (c i) -> p c j i", i=4))
+            nc.scalar.activation(grouped[:, cut:, :].rearrange("p (c i) j -> p c j i", i=4), x_raw[i][:, :, cut:].rearrange("p j (c i) -> p c j i", i=4), COPY)
             nc.vector.quantize_mx(
                 out=x_codes[:, t0 : t0 + width].bitcast(FP8X4),
                 scales=x_scales[:, t0 : t0 + width],
@@ -94,33 +92,47 @@ def tile_moe_tk_lin_relu_kernel(tc, xT, w_words, w_scales, b, gate, offs, pos1, 
             t0 += width
 
         y = [keep.tile([P, E * C], F32, name=f"y{h}") for h in range(H)]
-        e0 = 0
-        for i, experts in enumerate(GATHERS):
+        def gather(i, e0, experts):
             cols = experts * C
             codes = keep.tile([P, cols], U32, name=f"codes{i}", align_bytes=64)
             scales = keep.tile([P, cols], U8, name=f"scales{i}", align_bytes=64)
             slots = offs_t[:, e0 * C // 16 : (e0 + experts) * C // 16]
             nc.vector.tensor_copy(codes[:], x_codes[:].indirect(slots))
             nc.vector.tensor_copy(scales[:], x_scales[:].indirect(slots))
-            for h in range(H):
-                for s0 in range(0, experts, 3 if experts % 3 == 0 else 4):
-                    run = range(s0, min(experts, s0 + (3 if experts % 3 == 0 else 4)))
-                    acc = psum.tile([P, 512], F32, name="bank")
-                    for s in run:
-                        e = e0 + s
-                        nc.tensor.matmul_mx(
-                            out=acc[:, (s - s0) * C : (s - s0 + 1) * C],
-                            lhsT=w_t[e // W_GROUP][:, e % W_GROUP, h * P : (h + 1) * P].bitcast(FP8X4),
-                            lhsT_scale=w_sc[:, e, h * P : (h + 1) * P],
-                            rhs=codes[:, s * C : (s + 1) * C].bitcast(FP8X4),
-                            rhs_scale=scales[:, s * C : (s + 1) * C],
-                            start=True,
-                            stop=True,
-                        )
-                    for s in run:
-                        e = e0 + s
-                        nc.scalar.activation(y[h][:, e * C : (e + 1) * C], acc[:, (s - s0) * C : (s - s0 + 1) * C], RELU, bias=bias[:, h, e : e + 1])
+            return codes, scales
+
+        def multiply(h, e0, experts, codes, scales):
+            step = 3 if experts % 3 == 0 else 4
+            for s0 in range(0, experts, step):
+                run = range(s0, min(experts, s0 + step))
+                acc = psum.tile([P, 512], F32, name="bank")
+                for s in run:
+                    e = e0 + s
+                    nc.tensor.matmul_mx(
+                        out=acc[:, (s - s0) * C : (s - s0 + 1) * C],
+                        lhsT=w_t[e // W_GROUP][:, e % W_GROUP, h * P : (h + 1) * P].bitcast(FP8X4),
+                        lhsT_scale=w_sc[:, e, h * P : (h + 1) * P],
+                        rhs=codes[:, s * C : (s + 1) * C].bitcast(FP8X4),
+                        rhs_scale=scales[:, s * C : (s + 1) * C],
+                        start=True,
+                        stop=True,
+                    )
+                for s in run:
+                    e = e0 + s
+                    nc.scalar.activation(y[h][:, e * C : (e + 1) * C], acc[:, (s - s0) * C : (s - s0 + 1) * C], RELU, bias=bias[:, h, e : e + 1])
+
+        e0 = 0
+        late = []
+        for i, experts in enumerate(GATHERS):
+            codes, scales = gather(i, e0, experts)
+            multiply(0, e0, experts, codes, scales)
+            if i < len(GATHERS) - 2:
+                multiply(1, e0, experts, codes, scales)
+            else:
+                late.append((e0, experts, codes, scales))
             e0 += experts
+        for args in late:
+            multiply(1, *args)
 
         for h in range(H):
             prod = [keep.tile([P, T], F32, name=f"prod{h}{r}") for r in range(R)]
@@ -145,18 +157,41 @@ def tile_moe_tk_lin_relu_kernel(tc, xT, w_words, w_scales, b, gate, offs, pos1, 
                 nc.scalar.activation(result[:, lo:hi], back[:, : hi - lo], COPY)
                 store(lo, hi)
 
-            edge = T if h == 0 else 768
+            if h == 0:
+                product(0, 0, T)
+                product(1, 0, T)
+                for lo in range(0, T, 512):
+                    product(2, lo, lo + 512)
+                    tensor_sum(lo, lo + 512)
+                continue
+            edge = 768
+            turned = [psum.tile([P, 512], F32, name="bank") for j in range(edge // P)]
+            sums = keep.tile([P, edge], F32, name="sums_last")
+
+            def turn(r, lo, hi):
+                for j in range(lo // P, hi // P):
+                    nc.tensor.matmul(turned[j][:, :P], lhsT=prod[r][:, j * P : (j + 1) * P], rhs=ident[:], is_transpose=True, start=(r == 0), stop=(r == R - 1))
+
             for r in range(2):
                 product(r, 0, edge)
-            cuts = [0, 512, edge]
-            for lo, hi in zip(cuts[:-1], cuts[1:]):
+                turn(r, 0, edge)
+            pieces = ((0, 512), (512, edge))
+            for lo, hi in pieces:
                 product(2, lo, hi)
-                tensor_sum(lo, hi)
-            if h == 1:
-                half_sum = keep.tile([P, T - edge], F32, name="half_sum")
-                product(0, edge, T)
-                product(1, edge, T)
-                product(2, edge, T)
-                nc.vector.tensor_tensor(half_sum[:], prod[0][:, edge:], prod[1][:, edge:], ADD)
-                nc.vector.tensor_tensor(result[:, edge:], half_sum[:], prod[2][:, edge:], ADD)
-                store(edge, T)
+                turn(2, lo, hi)
+                for j in range(lo // P, hi // P):
+                    nc.scalar.activation(sums[:, j * P : (j + 1) * P], turned[j][:, :P], COPY)
+            for lo, hi in pieces:
+                back = psum.tile([P, 512], F32, name="bank")
+                for j in range(lo // P, hi // P):
+                    nc.tensor.transpose(back[:, j * P - lo : (j + 1) * P - lo], sums[:, j * P : (j + 1) * P], ident[:])
+                nc.scalar.activation(result[:, lo:hi], back[:, : hi - lo], COPY)
+                store(lo, hi)
+            half_sum = keep.tile([P, T - edge], F32, name="half_sum")
+            for r in range(R):
+                product(r, edge, T)
+            for lo in range(edge, T, P):
+                nc.vector.tensor_tensor(half_sum[:, lo - edge : lo - edge + P], prod[0][:, lo : lo + P], prod[1][:, lo : lo + P], ADD)
+            for lo in range(edge, T, P):
+                nc.vector.tensor_tensor(result[:, lo : lo + P], half_sum[:, lo - edge : lo - edge + P], prod[2][:, lo : lo + P], ADD)
+            store(edge, T)

from contextlib import ExitStack

import concourse.mybir as mybir
from concourse.masks import make_identity

K, T, E, C, N, R = 512, 1024, 24, 128, 256, 3
FLOPS = 2 * K * N * E * C
P = 128
H = N // P

F32 = mybir.dt.float32
BF16 = mybir.dt.bfloat16
U32 = mybir.dt.uint32
I32 = mybir.dt.int32
U16 = mybir.dt.uint16
U8 = mybir.dt.uint8
FP8X4 = mybir.dt.float8_e4m3fn_x4
MULT = mybir.AluOpType.mult
ADD = mybir.AluOpType.add
COPY = mybir.ActivationFunctionType.Copy
RELU = mybir.ActivationFunctionType.Relu

X_CHUNKS = (256, 512, 256)
SCALAR_SHARE = (64, 144, 64)
W_GROUP = 4
GATHERS = (6, 6, 6, 5, 1)


def tile_moe_tk_lin_relu_kernel(tc, xT, w_words, w_scales, b, gate, offs, pos1, pos2, pos3, out):
    nc = tc.nc
    with ExitStack() as ctx:
        lists = ctx.enter_context(tc.tile_pool(name="lists", bufs=1))
        keep = ctx.enter_context(tc.tile_pool(name="keep", bufs=1))
        psum = ctx.enter_context(tc.psum_pool(name="psum", bufs=8))

        offs_t = lists.tile([P, R * T // 16], U16, name="offs_t")
        pos_t = [lists.tile([P, T // 16], U16, name=f"pos{r}_t") for r in range(R)]

        w_sc = keep.tile([P, E, N], U8, name="w_sc", align_bytes=64)
        x_codes = keep.tile([P, T], U32, name="x_codes", align_bytes=64)
        x_scales = keep.tile([P, T], U8, name="x_scales", align_bytes=64)
        bias = keep.tile([P, H, E], F32, name="bias")
        warm = keep.tile([P, 1], F32, name="warm")
        ident = keep.tile([P, P], F32, name="ident")

        nc.vector.memset(warm[:], 0.0)
        nc.scalar.activation(warm[:], warm[:], RELU)
        nc.vector.memset(w_sc[:].rearrange("p e n -> p (e n)").bitcast(I32), 0)
        nc.gpsimd.memset(x_scales[:], 0)
        make_identity(nc, ident[:])

        x_view = xT.rearrange("(p j) t -> p j t", j=4)
        x_raw = []
        t0 = 0
        for i, width in enumerate(X_CHUNKS):
            raw = keep.tile([P, 4, width], F32, name=f"x_raw{i}")
            nc.sync.dma_start(out=raw[:], in_=x_view[:, :, t0 : t0 + width])
            x_raw.append(raw)
            t0 += width
        nc.sync.dma_start(offs_t[:], offs)
        sc_view = w_scales.rearrange("e a q n -> q (e a) n")
        for q in range(4):
            nc.sync.dma_start(
                out=w_sc[32 * q : 32 * q + 4, :, :].rearrange("p e n -> p (e n)").bitcast(I32).rearrange("p (e n) -> p e n", e=E),
                in_=sc_view[4 * q : 4 * q + 4].bitcast(I32),
            )
        w_view = w_words.rearrange("e a p n r -> p (e a) (n r)")
        w_t = []
        for g in range(E // W_GROUP):
            wt = keep.tile([P, W_GROUP, N], I32, name=f"w{g}", align_bytes=64)
            nc.sync.dma_start(out=wt[:], in_=w_view[:, g * W_GROUP : (g + 1) * W_GROUP, :].bitcast(I32))
            w_t.append(wt)
            if g == 0:
                nc.sync.dma_start(out=bias[:], in_=b.rearrange("(h p) e -> p h e", p=P))
        gate_t = [keep.tile([P, R, T], F32, name=f"gate{h}") for h in range(H)]
        for r, pos in enumerate((pos1, pos2, pos3)):
            nc.sync.dma_start(pos_t[r][:], pos)
            nc.sync.dma_start(out=gate_t[0][:, r, :], in_=gate[r, 0:P, :])
        nc.sync.dma_start(out=gate_t[1][:], in_=gate[:, P:N, :].rearrange("r p t -> p r t"))

        t0 = 0
        for i, width in enumerate(X_CHUNKS):
            grouped = keep.tile([P, width, 4], BF16, name=f"grouped{i}", align_bytes=64)
            cut = width - SCALAR_SHARE[i]
            nc.vector.tensor_copy(out=grouped[:, :cut, :].rearrange("p (c i) j -> p c j i", i=4), in_=x_raw[i][:, :, :cut].rearrange("p j (c i) -> p c j i", i=4))
            nc.scalar.activation(grouped[:, cut:, :].rearrange("p (c i) j -> p c j i", i=4), x_raw[i][:, :, cut:].rearrange("p j (c i) -> p c j i", i=4), COPY)
            nc.vector.quantize_mx(
                out=x_codes[:, t0 : t0 + width].bitcast(FP8X4),
                scales=x_scales[:, t0 : t0 + width],
                in_=grouped[:].rearrange("p w j -> p (w j)"),
            )
            t0 += width

        y = [keep.tile([P, E * C], F32, name=f"y{h}") for h in range(H)]
        def gather(i, e0, experts):
            cols = experts * C
            codes = keep.tile([P, cols], U32, name=f"codes{i}", align_bytes=64)
            scales = keep.tile([P, cols], U8, name=f"scales{i}", align_bytes=64)
            slots = offs_t[:, e0 * C // 16 : (e0 + experts) * C // 16]
            nc.vector.tensor_copy(codes[:], x_codes[:].indirect(slots))
            nc.vector.tensor_copy(scales[:], x_scales[:].indirect(slots))
            return codes, scales

        def multiply(h, e0, experts, codes, scales):
            step = 3 if experts % 3 == 0 else 4
            for s0 in range(0, experts, step):
                run = range(s0, min(experts, s0 + step))
                acc = psum.tile([P, 512], F32, name="bank")
                for s in run:
                    e = e0 + s
                    nc.tensor.matmul_mx(
                        out=acc[:, (s - s0) * C : (s - s0 + 1) * C],
                        lhsT=w_t[e // W_GROUP][:, e % W_GROUP, h * P : (h + 1) * P].bitcast(FP8X4),
                        lhsT_scale=w_sc[:, e, h * P : (h + 1) * P],
                        rhs=codes[:, s * C : (s + 1) * C].bitcast(FP8X4),
                        rhs_scale=scales[:, s * C : (s + 1) * C],
                        start=True,
                        stop=True,
                    )
                for s in run:
                    e = e0 + s
                    nc.scalar.activation(y[h][:, e * C : (e + 1) * C], acc[:, (s - s0) * C : (s - s0 + 1) * C], RELU, bias=bias[:, h, e : e + 1])

        e0 = 0
        late = []
        for i, experts in enumerate(GATHERS):
            codes, scales = gather(i, e0, experts)
            multiply(0, e0, experts, codes, scales)
            if i < len(GATHERS) - 2:
                multiply(1, e0, experts, codes, scales)
            else:
                late.append((e0, experts, codes, scales))
            e0 += experts
        for args in late:
            multiply(1, *args)

        for h in range(H):
            prod = [keep.tile([P, T], F32, name=f"prod{h}{r}") for r in range(R)]
            result = keep.tile([P, T], F32, name=f"result{h}")

            def product(r, lo, hi):
                nc.vector.tensor_tensor(prod[r][:, lo:hi], y[h][:].indirect(pos_t[r][:, lo // 16 : hi // 16]), gate_t[h][:, r, lo:hi], MULT)

            def store(lo, hi):
                nc.sync.dma_start(out=out[h * P : (h + 1) * P, lo:hi], in_=result[:, lo:hi])

            def tensor_sum(lo, hi):
                turned = psum.tile([P, 512], F32, name="bank")
                for j in range(lo // P, hi // P):
                    for r in range(R):
                        nc.tensor.matmul(turned[:, j * P - lo : (j + 1) * P - lo], lhsT=prod[r][:, j * P : (j + 1) * P], rhs=ident[:], is_transpose=True, start=(r == 0), stop=(r == R - 1))
                sums = keep.tile([P, hi - lo], F32, name=f"sums{h}{lo}")
                nc.scalar.activation(sums[:], turned[:, : hi - lo], COPY)
                back = psum.tile([P, 512], F32, name="bank")
                for j in range((hi - lo) // P):
                    nc.tensor.transpose(back[:, j * P : (j + 1) * P], sums[:, j * P : (j + 1) * P], ident[:])
                nc.scalar.activation(result[:, lo:hi], back[:, : hi - lo], COPY)
                store(lo, hi)

            if h == 0:
                product(0, 0, T)
                product(1, 0, T)
                for lo in range(0, T, 512):
                    product(2, lo, lo + 512)
                    tensor_sum(lo, lo + 512)
                continue
            edge = 768
            turned = [psum.tile([P, 512], F32, name="bank") for j in range(edge // P)]
            sums = keep.tile([P, edge], F32, name="sums_last")

            def turn(r, lo, hi):
                for j in range(lo // P, hi // P):
                    nc.tensor.matmul(turned[j][:, :P], lhsT=prod[r][:, j * P : (j + 1) * P], rhs=ident[:], is_transpose=True, start=(r == 0), stop=(r == R - 1))

            for r in range(2):
                product(r, 0, edge)
                turn(r, 0, edge)
            pieces = ((0, 512), (512, edge))
            for lo, hi in pieces:
                product(2, lo, hi)
                turn(2, lo, hi)
                for j in range(lo // P, hi // P):
                    nc.scalar.activation(sums[:, j * P : (j + 1) * P], turned[j][:, :P], COPY)
            for lo, hi in pieces:
                back = psum.tile([P, 512], F32, name="bank")
                for j in range(lo // P, hi // P):
                    nc.tensor.transpose(back[:, j * P - lo : (j + 1) * P - lo], sums[:, j * P : (j + 1) * P], ident[:])
                nc.scalar.activation(result[:, lo:hi], back[:, : hi - lo], COPY)
                store(lo, hi)
            half_sum = keep.tile([P, T - edge], F32, name="half_sum")
            for r in range(R):
                product(r, edge, T)
            for lo in range(edge, T, P):
                nc.vector.tensor_tensor(half_sum[:, lo - edge : lo - edge + P], prod[0][:, lo : lo + P], prod[1][:, lo : lo + P], ADD)
            for lo in range(edge, T, P):
                nc.vector.tensor_tensor(result[:, lo : lo + P], half_sum[:, lo - edge : lo - edge + P], prod[2][:, lo : lo + P], ADD)
            store(edge, T)
